import numpy as np, ml_dtypes
CORES = [3,5,19,21,35,37,51,53,67,69]
N = 10
KT, C = 2, 64
def setup_inputs(rng):
    return {"x": rng.standard_normal((N, 128, KT * C), dtype=np.float32).astype(ml_dtypes.bfloat16)}
def setup_inputs_big(rng):
    d = setup_inputs(rng)
    for k in ("x",): d[k] = (d[k].astype(np.float32) * 1024.0).astype(d[k].dtype)
    return d
def setup_inputs_small(rng):
    d = setup_inputs(rng)
    for k in ("x",): d[k] = (d[k].astype(np.float32) * (1 / 1024.0)).astype(d[k].dtype)
    return d
def setup_inputs_apart(rng):
    d = setup_inputs(rng)
    f = (10.0 ** rng.permutation(np.linspace(-1.5, 1.5, N))).astype(np.float32).reshape(N, 1, 1)
    for k in ("x",): d[k] = (d[k].astype(np.float32) * f).astype(d[k].dtype)
    return d
def reference(x):
    X = x.astype(np.float64)
    y = np.full((N, C, N * C), np.nan)
    for r in range(N):
        for i in range(N):
            s = i
            if s != r: y[r][:, C * i:C * i + C] = sum(X[r][:, C * t:C * t + C].T @ X[s][:, C * t:C * t + C] for t in range(KT))
    return {"y": y.astype(ml_dtypes.bfloat16 if x.dtype != np.float64 else np.float64)}

@@ -1,0 +1,171 @@
+from concourse.bass import DstId, RemoteDMATransfer
+
+N = 10
+C = 64
+KT = 2
+XW = KT * C
+MODE = {1: "F", 2: "F", 3: "D", 4: "D"}
+SEND_ORDER = "HFD"
+LATE_ORDER = "DWH"
+NBANK = 8
+
+SCRATCH = {
+    "xd": ("dram", [128, XW], "bfloat16"),
+    "hd": ("dram", [128, XW], "bfloat16"),
+    "xs": ("sbuf", [128, XW], "bfloat16"),
+    "land": ("sbuf", [128, (N - 1) * XW], "bfloat16"),
+    "ybuf": ("sbuf", [128, N * C], "bfloat16"),
+}
+for _b in range(NBANK):
+    SCRATCH["ps%d" % _b] = ("psum", [128, 512], "float32")
+
+SEMAPHORES = ["ldd", "lds", "fin", "din", "pin", "win", "hin", "hout", "sent", "cp", "stored"]
+SEMAPHORES += ["m%d" % _b for _b in range(NBANK)]
+
+
+def _bits(m):
+    return bin(m).count("1")
+
+
+def rank_program(g, core, T, topo):
+    sem = T.sem
+    cores = list(T.cores)
+    chips = []
+    for c in cores:
+        if topo.chip(c) not in chips:
+            chips.append(topo.chip(c))
+    nch = len(chips)
+    if topo.chip(core) not in chips:
+        return
+    f_offs = [k for k in sorted(MODE) if MODE[k] == "F"]
+    rest = [k for k in sorted(MODE) if MODE[k] != "F"]
+    h_offs = [k for k in sorted(MODE) if MODE[k] == "H"]
+    nf = len(f_offs)
+
+    def back(dst, src):
+        return (chips.index(topo.chip(dst)) - chips.index(topo.chip(src))) % nch
+
+    def same_die(a, b):
+        return topo.die(a) == topo.die(b)
+
+    def slot(dst, src):
+        off = back(dst, src)
+        if off == 0:
+            return 2 * nf
+        if off in f_offs:
+            return f_offs.index(off) + (0 if same_die(dst, src) else nf)
+        return 2 * nf + 1 + 2 * rest.index(off) + (0 if same_die(dst, src) else 1)
+
+    def land(dst, src):
+        k = slot(dst, src)
+        return T.land[:, k * XW:(k + 1) * XW]
+
+    def did(dst):
+        rid, pid, _ = topo.addr(dst)
+        return DstId(rid=rid, pnc=pid)
+
+    def hand(dst, src):
+        idle = [c for c in range(topo.CORES_PER_CHIP * topo.CHIPS)
+                if topo.chip(c) == topo.chip(dst) and same_die(c, src) and c not in cores]
+        return idle[h_offs.index(back(dst, src))]
+
+    rank = T.rank_of(core)
+    if rank is None:
+        mine = [c for c in cores if topo.chip(c) == topo.chip(core)]
+        srcs = [s for s in cores if back(core, s) in h_offs and hand(core, s) == core]
+        if not srcs:
+            return
+        s = srcs[0]
+        m = topo.mask(core, mine[0]) & topo.mask(core, mine[1])
+        g.wait_ge(sem.hin, _bits(topo.mask(s, core)))
+        g.remote_dma_fused(
+            [RemoteDMATransfer(dst_ids=[did(d) for d in mine], dma_engine_mask=m, remote_sem=sem.hout,
+                               srcs=[T.hd[:, :]], dsts=[land(d, s) for d in mine], alu_op=0)], local_sem=sem.sent)
+        g.wait_ge(sem.sent, _bits(m))
+        return
+
+    others = [c for c in cores if c != core]
+    partner = [c for c in others if back(c, core) == 0][0]
+    away = [c for c in others if c != partner]
+    off_mask = topo.mask(core, away[0])
+    all_mask = topo.mask(core, partner)
+    chip_mask = all_mask & ~off_mask
+    n_off, n_chip, n_all = _bits(off_mask), _bits(chip_mask), _bits(all_mask)
+
+    sends = {
+        "F": ([(d, land(d, core)) for d in away if back(d, core) in f_offs and same_die(d, core)], sem.fin),
+        "D": ([(d, land(d, core)) for d in away if MODE[back(d, core)] == "D"], sem.din),
+        "H": ([(hand(d, core), T.hd[:, :]) for d in away if back(d, core) in h_offs and same_die(d, core)], sem.hin),
+    }
+    fin_srcs = [s for s in away if back(core, s) in f_offs and same_die(core, s)]
+    win_srcs = [s for s in away if back(core, s) in f_offs and not same_die(core, s)]
+    din_srcs = [s for s in away if MODE[back(core, s)] == "D"]
+    h_srcs = [s for s in away if back(core, s) in h_offs]
+
+    g.sync.dma_start(T.xd[:, :], T.x[:, :]).then_inc(sem.ldd, 16)
+    g.sync.dma_start(T.xs[:, :], T.x[:, :]).then_inc(sem.lds, 16)
+
+    sent = 0
+    g.wait_ge(sem.ldd, 16)
+    for way in SEND_ORDER:
+        dsts, rsem = sends[way]
+        if dsts:
+            for d, _ in dsts:
+                assert topo.may_write(core, d)
+            g.remote_dma_fused(
+                [RemoteDMATransfer(dst_ids=[did(d) for d, _ in dsts], dma_engine_mask=off_mask, remote_sem=rsem,
+                                   srcs=[T.xd[:, :]], dsts=[ap for _, ap in dsts], alu_op=0)],
+                local_sem=sem.sent)
+            sent += n_off
+    rid, pid, _ = topo.addr(partner)
+    g.remote_dma(out_ap=land(partner, core), in_ap=T.xd[:, :], remote_sem=sem.pin, local_sem=sem.sent,
+                 pid=pid, routing_id=rid, dma_engine_mask=chip_mask)
+    sent += n_chip
+    if fin_srcs:
+        g.wait_ge(sem.fin, n_off * nf)
+        g.remote_dma(out_ap=T.land[:, nf * XW:2 * nf * XW], in_ap=T.land[:, 0:nf * XW], remote_sem=sem.win,
+                     local_sem=sem.sent, pid=pid, routing_id=rid, dma_engine_mask=chip_mask)
+        sent += n_chip
+    g.wait_ge(sem.sent, sent)
+
+    groups = [(sem.pin, n_chip, [partner])]
+    if fin_srcs:
+        groups.append((sem.fin, n_off * nf, fin_srcs))
+    early = len(groups)
+    lategroups = {"D": (sem.din, n_off * len(din_srcs), din_srcs), "W": (sem.win, n_chip, win_srcs),
+                  "H": (sem.hout, n_all * len(h_srcs), h_srcs)}
+    groups += [lategroups[w] for w in LATE_ORDER if lategroups[w][2]]
+    late = sum(len(gr[2]) for gr in groups[early:])
+    free = NBANK - early
+    sizes = [len(gr[2]) for gr in groups[:early]] + [2] * max(0, late - free)
+    sizes += [1] * (late - 2 * max(0, late - free))
+
+    tq, vq = g.tensor, g.vector
+    tq.wait_ge(sem.lds, 16)
+    chunks = [[] for _ in sizes]
+    bank = 0
+    for rsem, cnt, srcs in groups:
+        tq.wait_ge(rsem, cnt)
+        for s in srcs:
+            if len(chunks[bank]) == sizes[bank]:
+                bank += 1
+            col = len(chunks[bank]) * C
+            chunks[bank].append((s, col))
+            k = slot(core, s)
+            for t in range(KT):
+                mm = tq.matmul(out=T["ps%d" % bank][0:C, col:col + C], lhsT=T.xs[:, t * C:(t + 1) * C],
+                               rhs=T.land[:, k * XW + t * C:k * XW + (t + 1) * C], start=(t == 0), stop=(t == KT - 1))
+            mm.then_inc(sem["m%d" % bank], 1)
+
+    vq.memset(T.ybuf[0:C, rank * C:(rank + 1) * C], 0.0).then_inc(sem.cp, 1)
+    done = 1
+    for b, chunk in enumerate(chunks):
+        vq.wait_ge(sem["m%d" % b], len(chunk))
+        for s, col in chunk:
+            i = T.rank_of(s)
+            vq.tensor_copy(out=T.ybuf[0:C, i * C:(i + 1) * C], in_=T["ps%d" % b][0:C, col:col + C]).then_inc(sem.cp, 1)
+            done += 1
+
+    g.sync.wait_ge(sem.cp, done)
+    g.sync.dma_start(T.y[:, :], T.ybuf[0:C, :]).then_inc(sem.stored, 16)
+    g.sync.wait_ge(sem.stored, 16)

@@ -4,14 +4,12 @@ N = 10
 C = 64
 KT = 2
 XW = KT * C
-MODE = {1: "F", 2: "F", 3: "D", 4: "D"}
-SEND_ORDER = "HFD"
-LATE_ORDER = "DWH"
+F_OFFS = (1, 2)
+D_OFFS = (3, 4)
 NBANK = 8
 
 SCRATCH = {
     "xd": ("dram", [128, XW], "bfloat16"),
-    "hd": ("dram", [128, XW], "bfloat16"),
     "xs": ("sbuf", [128, XW], "bfloat16"),
     "land": ("sbuf", [128, (N - 1) * XW], "bfloat16"),
     "ybuf": ("sbuf", [128, N * C], "bfloat16"),
@@ -19,8 +17,9 @@ SCRATCH = {
 for _b in range(NBANK):
     SCRATCH["ps%d" % _b] = ("psum", [128, 512], "float32")
 
-SEMAPHORES = ["ldd", "lds", "fin", "din", "pin", "win", "hin", "hout", "sent", "cp", "stored"]
-SEMAPHORES += ["m%d" % _b for _b in range(NBANK)]
+SEMAPHORES = ["ldd", "lds", "pin", "dla", "dlb", "sent", "cpe", "cpl", "cpw", "ste", "stl"]
+SEMAPHORES += ["fin%d" % _k for _k in F_OFFS] + ["win%d" % _k for _k in F_OFFS]
+SEMAPHORES += ["din%d" % _k for _k in D_OFFS[:-1]] + ["m%d" % _b for _b in range(NBANK)]
 
 
 def _bits(m):
@@ -28,6 +27,9 @@ def _bits(m):
 
 
 def rank_program(g, core, T, topo):
+    rank = T.rank_of(core)
+    if rank is None:
+        return
     sem = T.sem
     cores = list(T.cores)
     chips = []
@@ -35,12 +37,7 @@ def rank_program(g, core, T, topo):
         if topo.chip(c) not in chips:
             chips.append(topo.chip(c))
     nch = len(chips)
-    if topo.chip(core) not in chips:
-        return
-    f_offs = [k for k in sorted(MODE) if MODE[k] == "F"]
-    rest = [k for k in sorted(MODE) if MODE[k] != "F"]
-    h_offs = [k for k in sorted(MODE) if MODE[k] == "H"]
-    nf = len(f_offs)
+    nf = len(F_OFFS)
 
     def back(dst, src):
         return (chips.index(topo.chip(dst)) - chips.index(topo.chip(src))) % nch
@@ -52,93 +49,81 @@ def rank_program(g, core, T, topo):
         off = back(dst, src)
         if off == 0:
             return 2 * nf
-        if off in f_offs:
-            return f_offs.index(off) + (0 if same_die(dst, src) else nf)
-        return 2 * nf + 1 + 2 * rest.index(off) + (0 if same_die(dst, src) else 1)
+        if off in F_OFFS:
+            return F_OFFS.index(off) + (0 if same_die(dst, src) else nf)
+        return 2 * nf + 1 + 2 * D_OFFS.index(off) + (0 if same_die(dst, src) else 1)
 
-    def land(dst, src):
-        k = slot(dst, src)
+    def land(k):
         return T.land[:, k * XW:(k + 1) * XW]
 
-    def did(dst):
-        rid, pid, _ = topo.addr(dst)
-        return DstId(rid=rid, pnc=pid)
-
-    def hand(dst, src):
-        idle = [c for c in range(topo.CORES_PER_CHIP * topo.CHIPS)
-                if topo.chip(c) == topo.chip(dst) and same_die(c, src) and c not in cores]
-        return idle[h_offs.index(back(dst, src))]
-
-    rank = T.rank_of(core)
-    if rank is None:
-        mine = [c for c in cores if topo.chip(c) == topo.chip(core)]
-        srcs = [s for s in cores if back(core, s) in h_offs and hand(core, s) == core]
-        if not srcs:
-            return
-        s = srcs[0]
-        m = topo.mask(core, mine[0]) & topo.mask(core, mine[1])
-        g.wait_ge(sem.hin, _bits(topo.mask(s, core)))
-        g.remote_dma_fused(
-            [RemoteDMATransfer(dst_ids=[did(d) for d in mine], dma_engine_mask=m, remote_sem=sem.hout,
-                               srcs=[T.hd[:, :]], dsts=[land(d, s) for d in mine], alu_op=0)], local_sem=sem.sent)
-        g.wait_ge(sem.sent, _bits(m))
-        return
-
     others = [c for c in cores if c != core]
+    for c in others:
+        assert topo.may_write(core, c)
     partner = [c for c in others if back(c, core) == 0][0]
     away = [c for c in others if c != partner]
-    off_mask = topo.mask(core, away[0])
-    all_mask = topo.mask(core, partner)
-    chip_mask = all_mask & ~off_mask
-    n_off, n_chip, n_all = _bits(off_mask), _bits(chip_mask), _bits(all_mask)
 
-    sends = {
-        "F": ([(d, land(d, core)) for d in away if back(d, core) in f_offs and same_die(d, core)], sem.fin),
-        "D": ([(d, land(d, core)) for d in away if MODE[back(d, core)] == "D"], sem.din),
-        "H": ([(hand(d, core), T.hd[:, :]) for d in away if back(d, core) in h_offs and same_die(d, core)], sem.hin),
-    }
-    fin_srcs = [s for s in away if back(core, s) in f_offs and same_die(core, s)]
-    win_srcs = [s for s in away if back(core, s) in f_offs and not same_die(core, s)]
-    din_srcs = [s for s in away if MODE[back(core, s)] == "D"]
-    h_srcs = [s for s in away if back(core, s) in h_offs]
+    def ahead(k, same):
+        return [d for d in away if back(d, core) == k and same_die(d, core) == same][0]
+
+    def behind(k, same):
+        return [s for s in away if back(core, s) == k and same_die(core, s) == same][0]
+
+    off_mask = topo.mask(core, away[0])
+    chip_mask = topo.mask(core, partner) & ~off_mask
+    n_off, n_chip = _bits(off_mask), _bits(chip_mask)
 
     g.sync.dma_start(T.xd[:, :], T.x[:, :]).then_inc(sem.ldd, 16)
     g.sync.dma_start(T.xs[:, :], T.x[:, :]).then_inc(sem.lds, 16)
 
+    def xfer(dsts, mask, rsem):
+        ids = []
+        for d in dsts:
+            rid, pid, _ = topo.addr(d)
+            ids.append(DstId(rid=rid, pnc=pid))
+        return RemoteDMATransfer(dst_ids=ids, dma_engine_mask=mask, remote_sem=rsem, srcs=[T.xd[:, :]],
+                                 dsts=[land(slot(d, core)) for d in dsts], alu_op=0)
+
     sent = 0
     g.wait_ge(sem.ldd, 16)
-    for way in SEND_ORDER:
-        dsts, rsem = sends[way]
-        if dsts:
-            for d, _ in dsts:
-                assert topo.may_write(core, d)
-            g.remote_dma_fused(
-                [RemoteDMATransfer(dst_ids=[did(d) for d, _ in dsts], dma_engine_mask=off_mask, remote_sem=rsem,
-                                   srcs=[T.xd[:, :]], dsts=[ap for _, ap in dsts], alu_op=0)],
-                local_sem=sem.sent)
-            sent += n_off
+    for k in F_OFFS:
+        g.remote_dma_fused([xfer([ahead(k, True)], off_mask, sem["fin%d" % k])], local_sem=sem.sent)
+        sent += n_off
+    for i, k in enumerate(D_OFFS[:-1]):
+        trs = [xfer([ahead(k, True), ahead(k, False)], off_mask, sem["din%d" % k])]
+        sent += n_off
+        if i == 0:
+            trs.append(xfer([partner], chip_mask, sem.pin))
+            sent += n_chip
+        g.remote_dma_fused(trs, local_sem=sem.sent)
+    for same, rsem in ((True, sem.dla), (False, sem.dlb)):
+        g.remote_dma_fused([xfer([ahead(D_OFFS[-1], same)], off_mask, rsem)], local_sem=sem.sent)
+        sent += n_off
     rid, pid, _ = topo.addr(partner)
-    g.remote_dma(out_ap=land(partner, core), in_ap=T.xd[:, :], remote_sem=sem.pin, local_sem=sem.sent,
-                 pid=pid, routing_id=rid, dma_engine_mask=chip_mask)
-    sent += n_chip
-    if fin_srcs:
-        g.wait_ge(sem.fin, n_off * nf)
-        g.remote_dma(out_ap=T.land[:, nf * XW:2 * nf * XW], in_ap=T.land[:, 0:nf * XW], remote_sem=sem.win,
-                     local_sem=sem.sent, pid=pid, routing_id=rid, dma_engine_mask=chip_mask)
+    for i, k in enumerate(F_OFFS):
+        g.wait_ge(sem["fin%d" % k], n_off)
+        g.remote_dma(out_ap=land(nf + i), in_ap=land(i), remote_sem=sem["win%d" % k], local_sem=sem.sent,
+                     pid=pid, routing_id=rid, dma_engine_mask=chip_mask)
         sent += n_chip
     g.wait_ge(sem.sent, sent)
 
-    groups = [(sem.pin, n_chip, [partner])]
-    if fin_srcs:
-        groups.append((sem.fin, n_off * nf, fin_srcs))
-    early = len(groups)
-    lategroups = {"D": (sem.din, n_off * len(din_srcs), din_srcs), "W": (sem.win, n_chip, win_srcs),
-                  "H": (sem.hout, n_all * len(h_srcs), h_srcs)}
-    groups += [lategroups[w] for w in LATE_ORDER if lategroups[w][2]]
-    late = sum(len(gr[2]) for gr in groups[early:])
-    free = NBANK - early
-    sizes = [len(gr[2]) for gr in groups[:early]] + [2] * max(0, late - free)
-    sizes += [1] * (late - 2 * max(0, late - free))
+    groups = [(sem["fin%d" % k], n_off, [behind(k, True)]) for k in F_OFFS]
+    groups.append((sem.pin, n_chip, [partner]))
+    groups += [(sem["din%d" % k], 2 * n_off, [behind(k, True), behind(k, False)]) for k in D_OFFS[:-1]]
+    groups += [(sem["win%d" % k], n_chip, [behind(k, False)]) for k in F_OFFS[:-1]]
+    groups += [(sem.dla, n_off, [behind(D_OFFS[-1], True)]), (sem.dlb, n_off, [behind(D_OFFS[-1], False)])]
+    groups.append((sem["win%d" % F_OFFS[-1]], n_chip, [behind(F_OFFS[-1], False)]))
+    sizes = [N - 1 - (NBANK - 1)] + [1] * (NBANK - 1)
+    cls = {i: "cpe" for i in range(N)}
+    pair = sorted(T.rank_of(behind(D_OFFS[-1], same)) for same in (True, False))
+    assert pair[1] == pair[0] + 1
+    cls[pair[0]] = cls[pair[1]] = "cpl"
+    wlast = T.rank_of(behind(F_OFFS[-1], False))
+    cls[wlast] = "cpw"
+    count = {"cpe": 0, "cpl": 0, "cpw": 0}
+
+    def csem(i):
+        count[cls[i]] += 1
+        return sem[cls[i]]
 
     tq, vq = g.tensor, g.vector
     tq.wait_ge(sem.lds, 16)
@@ -157,15 +142,29 @@ def rank_program(g, core, T, topo):
                                rhs=T.land[:, k * XW + t * C:k * XW + (t + 1) * C], start=(t == 0), stop=(t == KT - 1))
             mm.then_inc(sem["m%d" % bank], 1)
 
-    vq.memset(T.ybuf[0:C, rank * C:(rank + 1) * C], 0.0).then_inc(sem.cp, 1)
-    done = 1
+    vq.memset(T.ybuf[0:C, rank * C:(rank + 1) * C], 0.0).then_inc(csem(rank), 1)
     for b, chunk in enumerate(chunks):
         vq.wait_ge(sem["m%d" % b], len(chunk))
         for s, col in chunk:
             i = T.rank_of(s)
-            vq.tensor_copy(out=T.ybuf[0:C, i * C:(i + 1) * C], in_=T["ps%d" % b][0:C, col:col + C]).then_inc(sem.cp, 1)
-            done += 1
+            vq.tensor_copy(out=T.ybuf[0:C, i * C:(i + 1) * C], in_=T["ps%d" % b][0:C, col:col + C]).then_inc(csem(i), 1)
 
-    g.sync.wait_ge(sem.cp, done)
-    g.sync.dma_start(T.y[:, :], T.ybuf[0:C, :]).then_inc(sem.stored, 16)
-    g.sync.wait_ge(sem.stored, 16)
+    def store(q, a, b, ssem):
+        q.dma_start(T.y[:, a * C:b * C], T.ybuf[0:C, a * C:b * C]).then_inc(ssem, 16)
+
+    runs = []
+    for i in range(N):
+        if cls[i] == "cpe":
+            if runs and runs[-1][1] == i:
+                runs[-1][1] = i + 1
+            else:
+                runs.append([i, i + 1])
+    g.scalar.wait_ge(sem.cpe, count["cpe"])
+    for a, b in runs:
+        store(g.scalar, a, b, sem.ste)
+    g.scalar.wait_ge(sem.cpw, count["cpw"])
+    store(g.scalar, wlast, wlast + 1, sem.ste)
+    g.scalar.wait_ge(sem.ste, 16 * (len(runs) + 1))
+    g.sync.wait_ge(sem.cpl, count["cpl"])
+    store(g.sync, pair[0], pair[1] + 1, sem.stl)
+    g.sync.wait_ge(sem.stl, 16)

from concourse.bass import DstId, RemoteDMATransfer

N = 10
C = 64
KT = 2
XW = KT * C
F_OFFS = (1, 2)
D_OFFS = (3, 4)
NBANK = 8

SCRATCH = {
    "xd": ("dram", [128, XW], "bfloat16"),
    "xs": ("sbuf", [128, XW], "bfloat16"),
    "land": ("sbuf", [128, (N - 1) * XW], "bfloat16"),
    "ybuf": ("sbuf", [128, N * C], "bfloat16"),
}
for _b in range(NBANK):
    SCRATCH["ps%d" % _b] = ("psum", [128, 512], "float32")

SEMAPHORES = ["ldd", "lds", "pin", "dla", "dlb", "sent", "cpe", "cpl", "cpw", "ste", "stl"]
SEMAPHORES += ["fin%d" % _k for _k in F_OFFS] + ["win%d" % _k for _k in F_OFFS]
SEMAPHORES += ["din%d" % _k for _k in D_OFFS[:-1]] + ["m%d" % _b for _b in range(NBANK)]


def _bits(m):
    return bin(m).count("1")


def rank_program(g, core, T, topo):
    rank = T.rank_of(core)
    if rank is None:
        return
    sem = T.sem
    cores = list(T.cores)
    chips = []
    for c in cores:
        if topo.chip(c) not in chips:
            chips.append(topo.chip(c))
    nch = len(chips)
    nf = len(F_OFFS)

    def back(dst, src):
        return (chips.index(topo.chip(dst)) - chips.index(topo.chip(src))) % nch

    def same_die(a, b):
        return topo.die(a) == topo.die(b)

    def slot(dst, src):
        off = back(dst, src)
        if off == 0:
            return 2 * nf
        if off in F_OFFS:
            return F_OFFS.index(off) + (0 if same_die(dst, src) else nf)
        return 2 * nf + 1 + 2 * D_OFFS.index(off) + (0 if same_die(dst, src) else 1)

    def land(k):
        return T.land[:, k * XW:(k + 1) * XW]

    others = [c for c in cores if c != core]
    for c in others:
        assert topo.may_write(core, c)
    partner = [c for c in others if back(c, core) == 0][0]
    away = [c for c in others if c != partner]

    def ahead(k, same):
        return [d for d in away if back(d, core) == k and same_die(d, core) == same][0]

    def behind(k, same):
        return [s for s in away if back(core, s) == k and same_die(core, s) == same][0]

    off_mask = topo.mask(core, away[0])
    chip_mask = topo.mask(core, partner) & ~off_mask
    n_off, n_chip = _bits(off_mask), _bits(chip_mask)

    g.sync.dma_start(T.xd[:, :], T.x[:, :]).then_inc(sem.ldd, 16)
    g.sync.dma_start(T.xs[:, :], T.x[:, :]).then_inc(sem.lds, 16)

    def xfer(dsts, mask, rsem):
        ids = []
        for d in dsts:
            rid, pid, _ = topo.addr(d)
            ids.append(DstId(rid=rid, pnc=pid))
        return RemoteDMATransfer(dst_ids=ids, dma_engine_mask=mask, remote_sem=rsem, srcs=[T.xd[:, :]],
                                 dsts=[land(slot(d, core)) for d in dsts], alu_op=0)

    sent = 0
    g.wait_ge(sem.ldd, 16)
    for k in F_OFFS:
        g.remote_dma_fused([xfer([ahead(k, True)], off_mask, sem["fin%d" % k])], local_sem=sem.sent)
        sent += n_off
    for i, k in enumerate(D_OFFS[:-1]):
        trs = [xfer([ahead(k, True), ahead(k, False)], off_mask, sem["din%d" % k])]
        sent += n_off
        if i == 0:
            trs.append(xfer([partner], chip_mask, sem.pin))
            sent += n_chip
        g.remote_dma_fused(trs, local_sem=sem.sent)
    for same, rsem in ((True, sem.dla), (False, sem.dlb)):
        g.remote_dma_fused([xfer([ahead(D_OFFS[-1], same)], off_mask, rsem)], local_sem=sem.sent)
        sent += n_off
    rid, pid, _ = topo.addr(partner)
    for i, k in enumerate(F_OFFS):
        g.wait_ge(sem["fin%d" % k], n_off)
        g.remote_dma(out_ap=land(nf + i), in_ap=land(i), remote_sem=sem["win%d" % k], local_sem=sem.sent,
                     pid=pid, routing_id=rid, dma_engine_mask=chip_mask)
        sent += n_chip
    g.wait_ge(sem.sent, sent)

    groups = [(sem["fin%d" % k], n_off, [behind(k, True)]) for k in F_OFFS]
    groups.append((sem.pin, n_chip, [partner]))
    groups += [(sem["din%d" % k], 2 * n_off, [behind(k, True), behind(k, False)]) for k in D_OFFS[:-1]]
    groups += [(sem["win%d" % k], n_chip, [behind(k, False)]) for k in F_OFFS[:-1]]
    groups += [(sem.dla, n_off, [behind(D_OFFS[-1], True)]), (sem.dlb, n_off, [behind(D_OFFS[-1], False)])]
    groups.append((sem["win%d" % F_OFFS[-1]], n_chip, [behind(F_OFFS[-1], False)]))
    sizes = [N - 1 - (NBANK - 1)] + [1] * (NBANK - 1)
    cls = {i: "cpe" for i in range(N)}
    pair = sorted(T.rank_of(behind(D_OFFS[-1], same)) for same in (True, False))
    assert pair[1] == pair[0] + 1
    cls[pair[0]] = cls[pair[1]] = "cpl"
    wlast = T.rank_of(behind(F_OFFS[-1], False))
    cls[wlast] = "cpw"
    count = {"cpe": 0, "cpl": 0, "cpw": 0}

    def csem(i):
        count[cls[i]] += 1
        return sem[cls[i]]

    tq, vq = g.tensor, g.vector
    tq.wait_ge(sem.lds, 16)
    chunks = [[] for _ in sizes]
    bank = 0
    for rsem, cnt, srcs in groups:
        tq.wait_ge(rsem, cnt)
        for s in srcs:
            if len(chunks[bank]) == sizes[bank]:
                bank += 1
            col = len(chunks[bank]) * C
            chunks[bank].append((s, col))
            k = slot(core, s)
            for t in range(KT):
                mm = tq.matmul(out=T["ps%d" % bank][0:C, col:col + C], lhsT=T.xs[:, t * C:(t + 1) * C],
                               rhs=T.land[:, k * XW + t * C:k * XW + (t + 1) * C], start=(t == 0), stop=(t == KT - 1))
            mm.then_inc(sem["m%d" % bank], 1)

    vq.memset(T.ybuf[0:C, rank * C:(rank + 1) * C], 0.0).then_inc(csem(rank), 1)
    for b, chunk in enumerate(chunks):
        vq.wait_ge(sem["m%d" % b], len(chunk))
        for s, col in chunk:
            i = T.rank_of(s)
            vq.tensor_copy(out=T.ybuf[0:C, i * C:(i + 1) * C], in_=T["ps%d" % b][0:C, col:col + C]).then_inc(csem(i), 1)

    def store(q, a, b, ssem):
        q.dma_start(T.y[:, a * C:b * C], T.ybuf[0:C, a * C:b * C]).then_inc(ssem, 16)

    runs = []
    for i in range(N):
        if cls[i] == "cpe":
            if runs and runs[-1][1] == i:
                runs[-1][1] = i + 1
            else:
                runs.append([i, i + 1])
    g.scalar.wait_ge(sem.cpe, count["cpe"])
    for a, b in runs:
        store(g.scalar, a, b, sem.ste)
    g.scalar.wait_ge(sem.cpw, count["cpw"])
    store(g.scalar, wlast, wlast + 1, sem.ste)
    g.scalar.wait_ge(sem.ste, 16 * (len(runs) + 1))
    g.sync.wait_ge(sem.cpl, count["cpl"])
    store(g.sync, pair[0], pair[1] + 1, sem.stl)
    g.sync.wait_ge(sem.stl, 16)
